import numpy as np
import ml_dtypes


def mxq(x, axis, fmt="e4m3"):
    dtype, down = {"e4m3": (ml_dtypes.float8_e4m3fn, 7), "e5m2": (ml_dtypes.float8_e5m2, 14)}[fmt]
    v = np.moveaxis(np.asarray(x, np.float32).astype(ml_dtypes.bfloat16).astype(np.float64), axis, -1)
    blocks = v.reshape(v.shape[:-1] + (-1, 32))
    amax = np.abs(blocks).max(-1, keepdims=True)
    byte = np.maximum(np.where(amax > 0, np.frexp(amax)[1] - 1 + 127, 0) - down, 1)
    scale = np.exp2(byte - 127.0)
    codes = (blocks / scale).astype(np.float32).astype(dtype).astype(np.float64)
    return np.moveaxis((codes * scale).reshape(v.shape), -1, axis)


WIDE = False


def mx_kscale(k):
    if not WIDE:
        return np.ones(k)
    levels = np.array([30, -30])
    if k % 512:
        return np.exp2(np.random.permutation(np.resize(levels, k // 32))).repeat(32)
    a = np.empty((k // 512, 16))
    for p in range(k // 512):
        a[p, :8] = np.random.permutation(np.resize(levels, 8))
        for g in range(8):
            far = levels[np.abs(levels - a[p, g]) >= 10]
            a[p, g + 8] = far[np.random.randint(len(far))]
    return np.exp2(a.ravel()).repeat(32)


BF16 = ml_dtypes.bfloat16


def bf(x):
    return np.asarray(x, np.float32).astype(BF16)


def f64(x):
    return np.asarray(x).astype(np.float64)


E2M1 = np.array([0.0, 0.5, 1.0, 1.5, 2.0, 3.0, 4.0, 6.0, -0.0, -0.5, -1.0, -1.5, -2.0, -3.0, -4.0, -6.0])


def pack_weight(w, fmt):
    k, n = w.shape
    w = f64(bf(w)).reshape(k // 32, 32, n)
    amax = np.abs(w).max(1)
    if fmt == "e4m3":
        byte = np.frexp(amax)[1] - 1 + 127 - 7
    else:
        mant, ex = np.frexp(amax / 6.0)
        byte = np.where(mant > 0.5, ex, ex - 1) + 127
    byte = np.clip(np.where(amax > 0, byte, 1), 1, 254)
    scaled = (w * np.exp2(127.0 - byte)[:, None, :]).reshape(k, n).astype(np.float32)
    by_word = np.ascontiguousarray(scaled.reshape(k // 512, 128, 4, n).transpose(0, 1, 3, 2))
    if fmt == "e4m3":
        words = by_word.astype(ml_dtypes.float8_e4m3fn).view(np.uint8)
    else:
        c = by_word.astype(ml_dtypes.float4_e2m1fn).view(np.uint8) & 0xF
        words = c[..., 0::2] | (c[..., 1::2] << 4)
    return np.ascontiguousarray(words), np.ascontiguousarray(byte.astype(np.uint8).reshape(k // 512, 16, n))


def unpack_weight(words, scales, fmt):
    g, p, n, _ = words.shape
    if fmt == "e4m3":
        vals = np.ascontiguousarray(words).view(ml_dtypes.float8_e4m3fn).astype(np.float64)
    else:
        nib = np.empty((g, p, n, 4), np.uint8)
        nib[..., 0::2] = words & 0xF
        nib[..., 1::2] = words >> 4
        vals = E2M1[nib]
    vals = vals * np.repeat(np.exp2(scales.astype(np.float64) - 127.0), 8, axis=1)[..., None]
    return vals.transpose(0, 1, 3, 2).reshape(g * 512, n)
def pack4(w):
    words, scales = pack_weight(w, "e2m1")
    return words.reshape(words.shape[0], 128, -1), scales


def unpack4(words, scales):
    return unpack_weight(words.reshape(words.shape[0], 128, -1, 2), scales, "e2m1")


M, K, N = 1024, 1024, 2048


def setup_inputs():
    s, t = mx_kscale(K), mx_kscale(N)
    taps = np.random.standard_normal(N) / np.sqrt(K)
    shift = np.arange(N)[None, :] - (N // K) * np.arange(K)[:, None]
    h = taps[shift % N]
    h_words, h_scales = pack4(h / s[:, None])
    return {"lam": bf(np.random.standard_normal((M, K))),
            "amp": bf((1 + 0.1 * np.random.standard_normal(K)) * s),
            "h_words": h_words,
            "h_scales": h_scales,
            "y": bf(np.random.standard_normal((M, N))),
            "v": bf((1 + 0.1 * np.random.standard_normal(N)) * t),
            "f": bf(np.random.standard_normal((N, K)) / np.sqrt(N) / t[:, None])}


def reference(lam, amp, h_words, h_scales, y, v, f):
    h = unpack4(h_words, h_scales)
    x = np.tanh(f64(lam)) * f64(amp)
    z = mxq(x, 1, "e4m3") @ h
    r = (f64(y) - z) * f64(v)
    d = mxq(r, 1, "e5m2") @ mxq(f64(f), 0, "e4m3")
    return f64(lam) + d

@@ -1,0 +1,316 @@
+from contextlib import ExitStack
+
+import concourse.mybir as mybir
+from concourse.masks import make_identity
+
+F32 = mybir.dt.float32
+BF16 = mybir.dt.bfloat16
+I32 = mybir.dt.int32
+U32 = mybir.dt.uint32
+U8 = mybir.dt.uint8
+E4M3X4 = mybir.dt.float8_e4m3fn_x4
+E5M2X4 = mybir.dt.float8_e5m2_x4
+E2M1X4 = mybir.dt.float4_e2m1fn_x4
+ALU = mybir.AluOpType
+TANH = mybir.ActivationFunctionType.Tanh
+
+M, K, N = 1024, 1024, 2048
+P = 128
+FLOPS = 2 * M * K * N * 2
+TILES = M // P
+KG = K // 512
+NG = N // 512
+X_ON_V = 1
+FQ_LAG = 5
+S2_PLAN = {3: ((0, 0), (1, 0)), 4: ((2, 0),), 5: ((0, 1), (3, 0), (1, 1)), 6: ((2, 1), (4, 0), (3, 1)), 7: ((4, 1), (5, 0), (5, 1)), 8: ((6, 0), (6, 1)), 9: ((7, 0), (7, 1))}
+G_BLOCK = 3
+
+
+def tile_ftn_residual_turn_s9_kernel(tc, lam, amp, h_words, h_scales, y, v, f, out):
+    nc = tc.nc
+    with ExitStack() as ctx:
+        keep = ctx.enter_context(tc.tile_pool(name="keep", bufs=1))
+        work = ctx.enter_context(tc.tile_pool(name="work", bufs=2))
+        psum = ctx.enter_context(tc.psum_pool(name="psum", bufs=2))
+
+        warm = keep.tile([P, 1], F32)
+        nc.vector.memset(warm[:], 0.0)
+        warm_out = keep.tile([P, 1], F32)
+        nc.scalar.activation(out=warm_out[:], in_=warm[:], func=TANH)
+        hs = keep.tile([P, KG, N], U8, align_bytes=64)
+        nc.vector.memset(hs[:].rearrange("p g n -> p (g n)").bitcast(I32), 0)
+        ident = keep.tile([P, P], F32, align_bytes=64)
+        make_identity(nc, ident[:])
+
+        amp_sb = keep.tile([P, KG, 4], BF16, align_bytes=64)
+        v_sb = keep.tile([P, N], BF16, align_bytes=64)
+        hw = keep.tile([P, KG, 2 * N], U8, align_bytes=64)
+        lam_sb = keep.tile([P, TILES, K], BF16, align_bytes=64)
+        f_raw = keep.tile([P, 2, NG, 4, 512], BF16, align_bytes=64)
+
+        y_t = {}
+
+        def load_lam(i):
+            nc.sync.dma_start(out=lam_sb[:, i, :], in_=lam[P * i : P * (i + 1), :])
+
+        def load_y(i):
+            y_t[i] = work.tile([P, N], BF16, name="y_in", bufs=8, align_bytes=64)
+            nc.sync.dma_start(out=y_t[i][:], in_=y[P * i : P * (i + 1), :])
+
+        def load_f(kh, g):
+            cols = slice(512 * kh, 512 * (kh + 1))
+            nc.sync.dma_start(
+                out=f_raw[:, kh, g], in_=f[512 * g : 512 * (g + 1), cols].rearrange("(p j) k -> p j k", j=4)
+            )
+
+        def load_h(half):
+            cols = slice(N * half, N * (half + 1))
+            nc.sync.dma_start(
+                out=hw[:, :, cols].bitcast(I32), in_=h_words[:, :, cols].rearrange("g p c -> p g c").bitcast(I32)
+            )
+
+        nc.scalar.dma_start(out=amp_sb[:], in_=amp.rearrange("(g p t) -> p g t", g=KG, t=4))
+        load_lam(0)
+        load_lam(1)
+        for q in range(4):
+            nc.sync.dma_start(
+                out=hs[32 * q : 32 * q + 4].bitcast(I32),
+                in_=h_scales[:, 4 * q : 4 * q + 4, :].rearrange("g r n -> r g n").bitcast(I32),
+            )
+        load_h(0)
+        load_y(0)
+        load_h(1)
+        load_lam(2)
+        nc.sync.dma_start(out=v_sb[:], in_=v.partition_broadcast(P))
+        load_f(0, 0)
+        load_f(0, 1)
+        load_lam(3)
+        load_y(1)
+        load_f(0, 2)
+        load_f(0, 3)
+        load_y(2)
+        load_lam(4)
+        for g in range(NG):
+            load_f(1, g)
+        load_y(3)
+        for i in range(5, TILES):
+            load_lam(i)
+            load_y(i - 1)
+        load_y(TILES - 1)
+
+        f_codes = keep.tile([P, 2, NG, 512], U32, align_bytes=64)
+        f_scales = keep.tile([P, 2, NG, 512], U8, align_bytes=64)
+
+        xt, xf_t, xb_t, xc_t, xs_t = {}, {}, {}, {}, {}
+        z_t, t_t, r_t, rg_t, rc_t, rs_t, d_t, tr_t, fg_t = {}, {}, {}, {}, {}, {}, {}, {}, {}
+
+        def lam_turn(i):
+            bank = psum.tile([P, 4, P], F32, name="bank", tag="turn", bufs=2)
+            words = lam_sb[:, i, :].bitcast(F32)
+            for g in range(KG):
+                for u in range(2):
+                    nc.tensor.transpose(bank[:, 2 * g + u, :], words[:, 256 * g + u : 256 * (g + 1) : 2], ident[:])
+            xt[i] = bank
+
+        def lam_tanh(i):
+            xf = work.tile([P, KG, P, 4], F32, name="xf", bufs=2, align_bytes=64)
+            for g in range(KG):
+                nc.scalar.activation(
+                    out=xf[:, g].rearrange("p m (u e) -> p m u e", u=2),
+                    in_=xt[i][:, 2 * g : 2 * g + 2, :].bitcast(BF16).rearrange("p u (m e) -> p m u e", e=2),
+                    func=TANH,
+                )
+            xf_t[i] = xf
+
+        def x_mul(i):
+            engine = nc.vector if i < X_ON_V else nc.gpsimd
+            xb = work.tile([P, KG, P, 4], BF16, name="xb", bufs=1, align_bytes=64)
+            for g in range(KG):
+                engine.tensor_tensor(
+                    out=xb[:, g],
+                    in0=xf_t[i][:, g],
+                    in1=amp_sb[:, g, :].unsqueeze(1).to_broadcast([P, P, 4]),
+                    op=ALU.mult,
+                )
+            xb_t[i] = xb
+
+        def x_quant(i):
+            xc = work.tile([P, KG * P], U32, name="xc", bufs=3, align_bytes=64)
+            xs = work.tile([P, KG * P], U8, name="xs", bufs=3, align_bytes=64)
+            nc.vector.quantize_mx(
+                out=xc[:].bitcast(E4M3X4), scales=xs[:], in_=xb_t[i][:].rearrange("p g m t -> p (g m t)")
+            )
+            xc_t[i], xs_t[i] = xc, xs
+
+        def stage1(s):
+            i, b = divmod(s, NG)
+            z = psum.tile([P, 512], F32, name="z", tag="z", bufs=4)
+            for g in range(KG):
+                nc.tensor.matmul_mx(
+                    out=z[:],
+                    lhsT=xc_t[i][:, P * g : P * (g + 1)].bitcast(E4M3X4),
+                    lhsT_scale=xs_t[i][:, P * g : P * (g + 1)],
+                    rhs=hw[:, g, 1024 * b : 1024 * (b + 1)].bitcast(E2M1X4),
+                    rhs_scale=hs[:, g, 512 * b : 512 * (b + 1)],
+                    start=(g == 0),
+                    stop=(g == KG - 1),
+                )
+            z_t[s] = z
+
+        def sub(s):
+            i, b = divmod(s, NG)
+            if b == 0:
+                t_t[i] = work.tile([P, N], F32, name="t", bufs=5, align_bytes=64)
+            cols = slice(512 * b, 512 * (b + 1))
+            nc.vector.tensor_sub(out=t_t[i][:, cols], in0=y_t[i][:, cols], in1=z_t[s][:])
+
+        def mul(s):
+            i, b = divmod(s, NG)
+            if b == 0:
+                r_t[i] = work.tile([P, NG, 2, P, 2], BF16, name="r", bufs=2, align_bytes=64)
+            cols = slice(512 * b, 512 * (b + 1))
+            engine = nc.gpsimd if b == G_BLOCK and i < 0 else nc.vector
+            engine.tensor_tensor(
+                out=r_t[i][:, b],
+                in0=t_t[i][:, cols].rearrange("p (q u e) -> p u q e", u=2, e=2),
+                in1=v_sb[:, cols].rearrange("p (q u e) -> p u q e", u=2, e=2),
+                op=ALU.mult,
+            )
+
+        def r_turn(i, h):
+            bank = psum.tile([P, 4, P], F32, name="bank", tag="turn", bufs=2)
+            for g in range(2):
+                for u in range(2):
+                    words = r_t[i][:, 2 * h + g, u].rearrange("p q e -> p (q e)").bitcast(F32)
+                    nc.tensor.transpose(bank[:, 2 * g + u, :], words, ident[:])
+            tr_t[i, h] = bank
+
+        def r_copy(i, h):
+            if h == 0:
+                rg_t[i] = work.tile([P, NG, P, 4], BF16, name="rg", bufs=2, align_bytes=64)
+            nc.scalar.copy(
+                out=rg_t[i][:, 2 * h : 2 * h + 2].bitcast(F32),
+                in_=tr_t[i, h][:].rearrange("p (g u) m -> p g m u", u=2),
+            )
+
+        def r_quant(i):
+            rc = work.tile([P, NG * P], U32, name="rc", bufs=6, align_bytes=64)
+            rs = work.tile([P, NG * P], U8, name="rs", bufs=6, align_bytes=64)
+            nc.vector.quantize_mx(
+                out=rc[:].bitcast(E5M2X4), scales=rs[:], in_=rg_t[i][:].rearrange("p g m t -> p (g m t)")
+            )
+            rc_t[i], rs_t[i] = rc, rs
+
+        def f_copy(piece):
+            kg, q = divmod(piece, 2)
+            kh, g = divmod(kg, NG)
+            if q == 0:
+                fg_t[kg] = work.tile([P, 512, 4], BF16, name="fg", bufs=5, align_bytes=64)
+            c0 = 256 * q
+            nc.scalar.copy(
+                out=fg_t[kg][:, 256 * q : 256 * (q + 1), :],
+                in_=f_raw[:, kh, g, :, c0 : c0 + 256].rearrange("p j c -> p c j"),
+            )
+
+        def f_quant(kg):
+            kh, g = divmod(kg, NG)
+            nc.vector.quantize_mx(
+                out=f_codes[:, kh, g, :].bitcast(E4M3X4),
+                scales=f_scales[:, kh, g, :],
+                in_=fg_t[kg][:].rearrange("p c j -> p (c j)"),
+            )
+
+        def stage2(i, kh):
+            d = psum.tile([P, 512], F32, name="d", tag="d", bufs=2)
+            for g in range(NG):
+                nc.tensor.matmul_mx(
+                    out=d[:],
+                    lhsT=rc_t[i][:, P * g : P * (g + 1)].bitcast(E5M2X4),
+                    lhsT_scale=rs_t[i][:, P * g : P * (g + 1)],
+                    rhs=f_codes[:, kh, g, :].bitcast(E4M3X4),
+                    rhs_scale=f_scales[:, kh, g, :],
+                    start=(g == 0),
+                    stop=(g == NG - 1),
+                )
+            d_t[i, kh] = d
+
+        def add(i, kh):
+            o = work.tile([P, 512], F32, name="o", bufs=4, align_bytes=64)
+            cols = slice(512 * kh, 512 * (kh + 1))
+            nc.vector.tensor_add(out=o[:], in0=d_t[i, kh][:], in1=lam_sb[:, i, cols])
+            nc.sync.dma_start(out=out[P * i : P * (i + 1), cols], in_=o[:])
+
+        f_done = [0, 0]
+
+        def f_step(copies, quants):
+            for n in range(copies):
+                if f_done[0] < 16:
+                    f_copy(f_done[0])
+                    f_done[0] += 1
+            for n in range(quants):
+                if 2 * f_done[1] + FQ_LAG < f_done[0] or (f_done[0] == 16 and f_done[1] < 8):
+                    f_quant(f_done[1])
+                    f_done[1] += 1
+
+        lam_turn(0)
+        lam_turn(1)
+        lam_tanh(0)
+        lam_tanh(1)
+        x_mul(0)
+        x_quant(0)
+        x_mul(1)
+        for s in range(NG):
+            stage1(s)
+        lam_turn(2)
+        lam_tanh(2)
+        adds = []
+        for i in range(TILES + 2):
+            s2 = S2_PLAN.get(i, ())
+            if 1 <= i < TILES - 1:
+                x_quant(i + 1)
+            if 1 <= i < TILES - 2:
+                x_mul(i + 2)
+            for b in range(NG):
+                if i < TILES:
+                    sub(NG * i + b)
+                if 1 <= i < TILES - 1:
+                    stage1(NG * (i + 1) + b)
+            if i == 0:
+                x_quant(1)
+                x_mul(2)
+                for b in range(NG):
+                    stage1(NG + b)
+            for x in adds:
+                add(*x)
+            adds = []
+            if 1 <= i <= TILES - 1:
+                mul(NG * (i - 1) + 3)
+            if 1 <= i <= TILES:
+                r_turn(i - 1, 1)
+                r_copy(i - 1, 1)
+            f_step(1, 1)
+            if i + 3 < TILES:
+                lam_turn(i + 3)
+                lam_tanh(i + 3)
+            f_step(1, 0)
+            for x in s2[:1]:
+                stage2(*x)
+                adds.append(x)
+            if i < TILES:
+                mul(NG * i)
+                mul(NG * i + 1)
+                r_turn(i, 0)
+                r_copy(i, 0)
+                f_step(2, 1)
+                mul(NG * i + 2)
+            if i == TILES - 1:
+                mul(NG * i + 3)
+            if 1 <= i <= TILES:
+                r_quant(i - 1)
+            for x in s2[1:]:
+                if len(adds) == 2:
+                    add(*adds.pop(0))
+                stage2(*x)
+                adds.append(x)
+        for x in adds:
+            add(*x)

@@ -22,8 +22,11 @@ KG = K // 512
 NG = N // 512
 X_ON_V = 1
 FQ_LAG = 5
-S2_PLAN = {3: ((0, 0), (1, 0)), 4: ((2, 0),), 5: ((0, 1), (3, 0), (1, 1)), 6: ((2, 1), (4, 0), (3, 1)), 7: ((4, 1), (5, 0), (5, 1)), 8: ((6, 0), (6, 1)), 9: ((7, 0), (7, 1))}
-G_BLOCK = 3
+F_ON_G = ()
+F_ON_V = ()
+C_TILES = 4
+G_BLOCKS = (1, 3)
+F_STEPS = (1, 1, 1, 1)
 
 
 def tile_ftn_residual_turn_s9_kernel(tc, lam, amp, h_words, h_scales, y, v, f, out):
@@ -42,6 +45,7 @@ def tile_ftn_residual_turn_s9_kernel(tc, lam, amp, h_words, h_scales, y, v, f, o
         ident = keep.tile([P, P], F32, align_bytes=64)
         make_identity(nc, ident[:])
 
+        v_turned = keep.tile([P, NG, 4], BF16, align_bytes=64)
         amp_sb = keep.tile([P, KG, 4], BF16, align_bytes=64)
         v_sb = keep.tile([P, N], BF16, align_bytes=64)
         hw = keep.tile([P, KG, 2 * N], U8, align_bytes=64)
@@ -80,8 +84,8 @@ def tile_ftn_residual_turn_s9_kernel(tc, lam, amp, h_words, h_scales, y, v, f, o
         load_h(0)
         load_y(0)
         load_h(1)
+        nc.sync.dma_start(out=v_turned[:], in_=v.rearrange("(g p t) -> p g t", g=NG, t=4))
         load_lam(2)
-        nc.sync.dma_start(out=v_sb[:], in_=v.partition_broadcast(P))
         load_f(0, 0)
         load_f(0, 1)
         load_lam(3)
@@ -93,6 +97,7 @@ def tile_ftn_residual_turn_s9_kernel(tc, lam, amp, h_words, h_scales, y, v, f, o
         for g in range(NG):
             load_f(1, g)
         load_y(3)
+        nc.sync.dma_start(out=v_sb[:], in_=v.partition_broadcast(P))
         for i in range(5, TILES):
             load_lam(i)
             load_y(i - 1)
@@ -162,18 +167,41 @@ def tile_ftn_residual_turn_s9_kernel(tc, lam, amp, h_words, h_scales, y, v, f, o
             if b == 0:
                 t_t[i] = work.tile([P, N], F32, name="t", bufs=5, align_bytes=64)
             cols = slice(512 * b, 512 * (b + 1))
-            nc.vector.tensor_sub(out=t_t[i][:, cols], in0=y_t[i][:, cols], in1=z_t[s][:])
+            if i < C_TILES:
+                nc.vector.tensor_sub(
+                    out=t_t[i][:, cols].rearrange("p (t q) -> p t q", t=4),
+                    in0=y_t[i][:, cols].rearrange("p (q t) -> p t q", t=4),
+                    in1=z_t[s][:].rearrange("p (q t) -> p t q", t=4),
+                )
+            else:
+                nc.vector.tensor_sub(out=t_t[i][:, cols], in0=y_t[i][:, cols], in1=z_t[s][:])
 
         def mul(s):
             i, b = divmod(s, NG)
             if b == 0:
                 r_t[i] = work.tile([P, NG, 2, P, 2], BF16, name="r", bufs=2, align_bytes=64)
             cols = slice(512 * b, 512 * (b + 1))
-            engine = nc.gpsimd if b == G_BLOCK and i < 0 else nc.vector
+            engine = nc.gpsimd if b in G_BLOCKS else nc.vector
             engine.tensor_tensor(
                 out=r_t[i][:, b],
                 in0=t_t[i][:, cols].rearrange("p (q u e) -> p u q e", u=2, e=2),
                 in1=v_sb[:, cols].rearrange("p (q u e) -> p u q e", u=2, e=2),
+                op=ALU.mult,
+            )
+
+        def t_turn(i, b):
+            bank = psum.tile([P, 4, P], F32, name="bank", tag="turn", bufs=2)
+            for t in range(4):
+                nc.tensor.transpose(bank[:, t, :], t_t[i][:, 512 * b + P * t : 512 * b + P * (t + 1)], ident[:])
+            tr_t[i, b] = bank
+
+        def t_mul(i, b):
+            if b == 0:
+                rg_t[i] = work.tile([P, NG, P, 4], BF16, name="rg", bufs=2, align_bytes=64)
+            nc.vector.tensor_tensor(
+                out=rg_t[i][:, b],
+                in0=tr_t[i, b][:].rearrange("p t m -> p m t"),
+                in1=v_turned[:, b, :].unsqueeze(1).to_broadcast([P, P, 4]),
                 op=ALU.mult,
             )
 
@@ -206,11 +234,14 @@ def tile_ftn_residual_turn_s9_kernel(tc, lam, amp, h_words, h_scales, y, v, f, o
             kh, g = divmod(kg, NG)
             if q == 0:
                 fg_t[kg] = work.tile([P, 512, 4], BF16, name="fg", bufs=5, align_bytes=64)
-            c0 = 256 * q
-            nc.scalar.copy(
-                out=fg_t[kg][:, 256 * q : 256 * (q + 1), :],
-                in_=f_raw[:, kh, g, :, c0 : c0 + 256].rearrange("p j c -> p c j"),
-            )
+            dst = fg_t[kg][:, 256 * q : 256 * (q + 1), :]
+            src = f_raw[:, kh, g, :, 256 * q : 256 * (q + 1)].rearrange("p j c -> p c j")
+            if piece in F_ON_G:
+                nc.gpsimd.tensor_scalar(out=dst, in0=src, scalar1=1.0, scalar2=0.0, op0=ALU.mult, op1=ALU.add)
+            elif piece in F_ON_V:
+                nc.vector.tensor_copy(out=dst, in_=src)
+            else:
+                nc.scalar.copy(out=dst, in_=src)
 
         def f_quant(kg):
             kh, g = divmod(kg, NG)
@@ -252,6 +283,24 @@ def tile_ftn_residual_turn_s9_kernel(tc, lam, amp, h_words, h_scales, y, v, f, o
                     f_quant(f_done[1])
                     f_done[1] += 1
 
+        pending = []
+
+        todo = [(i, kh) for i in range(TILES) for kh in range(2)]
+
+        def second():
+            for x in todo:
+                if x[0] in rc_t and f_done[1] >= NG * (x[1] + 1):
+                    if len(pending) == 2:
+                        add(*pending.pop(0))
+                    stage2(*x)
+                    pending.append(x)
+                    todo.remove(x)
+                    break
+
+        def flush(keep_last=0):
+            while len(pending) > keep_last:
+                add(*pending.pop(0))
+
         lam_turn(0)
         lam_turn(1)
         lam_tanh(0)
@@ -263,9 +312,7 @@ def tile_ftn_residual_turn_s9_kernel(tc, lam, amp, h_words, h_scales, y, v, f, o
             stage1(s)
         lam_turn(2)
         lam_tanh(2)
-        adds = []
         for i in range(TILES + 2):
-            s2 = S2_PLAN.get(i, ())
             if 1 <= i < TILES - 1:
                 x_quant(i + 1)
             if 1 <= i < TILES - 2:
@@ -275,42 +322,49 @@ def tile_ftn_residual_turn_s9_kernel(tc, lam, amp, h_words, h_scales, y, v, f, o
                     sub(NG * i + b)
                 if 1 <= i < TILES - 1:
                     stage1(NG * (i + 1) + b)
+                if b == 1 and 1 <= i <= TILES:
+                    r_quant(i - 1)
             if i == 0:
                 x_quant(1)
                 x_mul(2)
                 for b in range(NG):
                     stage1(NG + b)
-            for x in adds:
-                add(*x)
-            adds = []
-            if 1 <= i <= TILES - 1:
-                mul(NG * (i - 1) + 3)
-            if 1 <= i <= TILES:
-                r_turn(i - 1, 1)
-                r_copy(i - 1, 1)
-            f_step(1, 1)
-            if i + 3 < TILES:
-                lam_turn(i + 3)
-                lam_tanh(i + 3)
-            f_step(1, 0)
-            for x in s2[:1]:
-                stage2(*x)
-                adds.append(x)
-            if i < TILES:
+            flush()
+            second()
+            f_step(F_STEPS[0], 1)
+            if i < C_TILES:
+                t_turn(i, 0)
+                t_turn(i, 1)
+                t_mul(i, 0)
+                t_turn(i, 2)
+                f_step(F_STEPS[1], 0)
+                t_mul(i, 1)
+                t_turn(i, 3)
+                t_mul(i, 2)
+                if i + 3 < TILES:
+                    lam_turn(i + 3)
+                    lam_tanh(i + 3)
+                second()
+                t_mul(i, 3)
+                f_step(F_STEPS[2], 1)
+            elif i < TILES:
                 mul(NG * i)
                 mul(NG * i + 1)
                 r_turn(i, 0)
                 r_copy(i, 0)
-                f_step(2, 1)
+                f_step(F_STEPS[1], 0)
+                if i + 3 < TILES:
+                    lam_turn(i + 3)
+                    lam_tanh(i + 3)
                 mul(NG * i + 2)
-            if i == TILES - 1:
+                flush(1)
+                second()
                 mul(NG * i + 3)
-            if 1 <= i <= TILES:
-                r_quant(i - 1)
-            for x in s2[1:]:
-                if len(adds) == 2:
-                    add(*adds.pop(0))
-                stage2(*x)
-                adds.append(x)
-        for x in adds:
-            add(*x)
+                r_turn(i, 1)
+                r_copy(i, 1)
+                f_step(F_STEPS[2], 1)
+            else:
+                second()
+            second()
+            f_step(F_STEPS[3], 0)
+        flush()

@@ -12,6 +12,7 @@ E4M3X4 = mybir.dt.float8_e4m3fn_x4
 E5M2X4 = mybir.dt.float8_e5m2_x4
 E2M1X4 = mybir.dt.float4_e2m1fn_x4
 ALU = mybir.AluOpType
+COPY = mybir.ActivationFunctionType.Copy
 TANH = mybir.ActivationFunctionType.Tanh
 
 M, K, N = 1024, 1024, 2048
@@ -20,12 +21,10 @@ FLOPS = 2 * M * K * N * 2
 TILES = M // P
 KG = K // 512
 NG = N // 512
-X_ON_V = 1
-FQ_LAG = 5
-F_ON_G = ()
+X_ON_V = 8
 F_ON_V = ()
-C_TILES = 4
-G_BLOCKS = (1, 3)
+TURN, Z = 3, 3
+S_BLOCKS = {3: (1, 3), 4: (0, 1, 2, 3), 5: (0, 1, 2, 3), 6: (0, 1, 2, 3), 7: (0, 1, 2, 3)}
 F_STEPS = (1, 1, 1, 1)
 
 
@@ -47,7 +46,6 @@ def tile_ftn_residual_turn_s9_kernel(tc, lam, amp, h_words, h_scales, y, v, f, o
 
         v_turned = keep.tile([P, NG, 4], BF16, align_bytes=64)
         amp_sb = keep.tile([P, KG, 4], BF16, align_bytes=64)
-        v_sb = keep.tile([P, N], BF16, align_bytes=64)
         hw = keep.tile([P, KG, 2 * N], U8, align_bytes=64)
         lam_sb = keep.tile([P, TILES, K], BF16, align_bytes=64)
         f_raw = keep.tile([P, 2, NG, 4, 512], BF16, align_bytes=64)
@@ -86,10 +84,10 @@ def tile_ftn_residual_turn_s9_kernel(tc, lam, amp, h_words, h_scales, y, v, f, o
         load_h(1)
         nc.sync.dma_start(out=v_turned[:], in_=v.rearrange("(g p t) -> p g t", g=NG, t=4))
         load_lam(2)
+        load_y(1)
         load_f(0, 0)
         load_f(0, 1)
         load_lam(3)
-        load_y(1)
         load_f(0, 2)
         load_f(0, 3)
         load_y(2)
@@ -97,20 +95,21 @@ def tile_ftn_residual_turn_s9_kernel(tc, lam, amp, h_words, h_scales, y, v, f, o
         for g in range(NG):
             load_f(1, g)
         load_y(3)
-        nc.sync.dma_start(out=v_sb[:], in_=v.partition_broadcast(P))
         for i in range(5, TILES):
             load_lam(i)
             load_y(i - 1)
         load_y(TILES - 1)
 
+        v_col = keep.tile([P, NG, 4], F32)
+        nc.vector.tensor_copy(out=v_col[:], in_=v_turned[:])
         f_codes = keep.tile([P, 2, NG, 512], U32, align_bytes=64)
         f_scales = keep.tile([P, 2, NG, 512], U8, align_bytes=64)
 
         xt, xf_t, xb_t, xc_t, xs_t = {}, {}, {}, {}, {}
-        z_t, t_t, r_t, rg_t, rc_t, rs_t, d_t, tr_t, fg_t = {}, {}, {}, {}, {}, {}, {}, {}, {}
+        z_t, t_t, rn_t, rg_t, rc_t, rs_t, d_t, tr_t, fg_t = {}, {}, {}, {}, {}, {}, {}, {}, {}
 
         def lam_turn(i):
-            bank = psum.tile([P, 4, P], F32, name="bank", tag="turn", bufs=2)
+            bank = psum.tile([P, 4, P], F32, name="bank", tag="turn", bufs=TURN)
             words = lam_sb[:, i, :].bitcast(F32)
             for g in range(KG):
                 for u in range(2):
@@ -149,7 +148,7 @@ def tile_ftn_residual_turn_s9_kernel(tc, lam, amp, h_words, h_scales, y, v, f, o
 
         def stage1(s):
             i, b = divmod(s, NG)
-            z = psum.tile([P, 512], F32, name="z", tag="z", bufs=4)
+            z = psum.tile([P, 512], F32, name="z", tag="z", bufs=Z)
             for g in range(KG):
                 nc.tensor.matmul_mx(
                     out=z[:],
@@ -167,59 +166,43 @@ def tile_ftn_residual_turn_s9_kernel(tc, lam, amp, h_words, h_scales, y, v, f, o
             if b == 0:
                 t_t[i] = work.tile([P, N], F32, name="t", bufs=5, align_bytes=64)
             cols = slice(512 * b, 512 * (b + 1))
-            if i < C_TILES:
-                nc.vector.tensor_sub(
-                    out=t_t[i][:, cols].rearrange("p (t q) -> p t q", t=4),
-                    in0=y_t[i][:, cols].rearrange("p (q t) -> p t q", t=4),
-                    in1=z_t[s][:].rearrange("p (q t) -> p t q", t=4),
-                )
-            else:
-                nc.vector.tensor_sub(out=t_t[i][:, cols], in0=y_t[i][:, cols], in1=z_t[s][:])
-
-        def mul(s):
-            i, b = divmod(s, NG)
-            if b == 0:
-                r_t[i] = work.tile([P, NG, 2, P, 2], BF16, name="r", bufs=2, align_bytes=64)
-            cols = slice(512 * b, 512 * (b + 1))
-            engine = nc.gpsimd if b in G_BLOCKS else nc.vector
-            engine.tensor_tensor(
-                out=r_t[i][:, b],
-                in0=t_t[i][:, cols].rearrange("p (q u e) -> p u q e", u=2, e=2),
-                in1=v_sb[:, cols].rearrange("p (q u e) -> p u q e", u=2, e=2),
-                op=ALU.mult,
+            nc.vector.tensor_sub(
+                out=t_t[i][:, cols].rearrange("p (t q) -> p t q", t=4),
+                in0=y_t[i][:, cols].rearrange("p (q t) -> p t q", t=4),
+                in1=z_t[s][:].rearrange("p (q t) -> p t q", t=4),
             )
 
-        def t_turn(i, b):
-            bank = psum.tile([P, 4, P], F32, name="bank", tag="turn", bufs=2)
+        def t_turn(s):
+            i, b = divmod(s, NG)
+            bank = psum.tile([P, 4, P], F32, name="bank", tag="turn", bufs=TURN)
             for t in range(4):
                 nc.tensor.transpose(bank[:, t, :], t_t[i][:, 512 * b + P * t : 512 * b + P * (t + 1)], ident[:])
             tr_t[i, b] = bank
 
-        def t_mul(i, b):
+        def t_scale(s):
+            i, b = divmod(s, NG)
+            if b in S_BLOCKS.get(i, ()):
+                rn = work.tile([P, 4, P], BF16, name="rn", bufs=3, align_bytes=64)
+                for t in range(4):
+                    nc.scalar.activation(out=rn[:, t, :], in_=tr_t[i, b][:, t, :], func=COPY, scale=v_col[:, b, t : t + 1])
+                rn_t[s] = rn
+
+        def t_mul(s):
+            i, b = divmod(s, NG)
             if b == 0:
                 rg_t[i] = work.tile([P, NG, P, 4], BF16, name="rg", bufs=2, align_bytes=64)
-            nc.vector.tensor_tensor(
-                out=rg_t[i][:, b],
-                in0=tr_t[i, b][:].rearrange("p t m -> p m t"),
-                in1=v_turned[:, b, :].unsqueeze(1).to_broadcast([P, P, 4]),
-                op=ALU.mult,
-            )
-
-        def r_turn(i, h):
-            bank = psum.tile([P, 4, P], F32, name="bank", tag="turn", bufs=2)
-            for g in range(2):
-                for u in range(2):
-                    words = r_t[i][:, 2 * h + g, u].rearrange("p q e -> p (q e)").bitcast(F32)
-                    nc.tensor.transpose(bank[:, 2 * g + u, :], words, ident[:])
-            tr_t[i, h] = bank
-
-        def r_copy(i, h):
-            if h == 0:
-                rg_t[i] = work.tile([P, NG, P, 4], BF16, name="rg", bufs=2, align_bytes=64)
-            nc.scalar.copy(
-                out=rg_t[i][:, 2 * h : 2 * h + 2].bitcast(F32),
-                in_=tr_t[i, h][:].rearrange("p (g u) m -> p g m u", u=2),
-            )
+            if s in rn_t:
+                nc.vector.tensor_copy(
+                    out=rg_t[i][:, b].rearrange("p (c i) t -> p c t i", i=4),
+                    in_=rn_t[s][:].rearrange("p t (c i) -> p c t i", i=4),
+                )
+            else:
+                nc.vector.tensor_tensor(
+                    out=rg_t[i][:, b],
+                    in0=tr_t[i, b][:].rearrange("p t m -> p m t"),
+                    in1=v_turned[:, b, :].unsqueeze(1).to_broadcast([P, P, 4]),
+                    op=ALU.mult,
+                )
 
         def r_quant(i):
             rc = work.tile([P, NG * P], U32, name="rc", bufs=6, align_bytes=64)
@@ -234,11 +217,9 @@ def tile_ftn_residual_turn_s9_kernel(tc, lam, amp, h_words, h_scales, y, v, f, o
             kh, g = divmod(kg, NG)
             if q == 0:
                 fg_t[kg] = work.tile([P, 512, 4], BF16, name="fg", bufs=5, align_bytes=64)
-            dst = fg_t[kg][:, 256 * q : 256 * (q + 1), :]
-            src = f_raw[:, kh, g, :, 256 * q : 256 * (q + 1)].rearrange("p j c -> p c j")
-            if piece in F_ON_G:
-                nc.gpsimd.tensor_scalar(out=dst, in0=src, scalar1=1.0, scalar2=0.0, op0=ALU.mult, op1=ALU.add)
-            elif piece in F_ON_V:
+            dst = fg_t[kg][:, 256 * q : 256 * (q + 1), :].rearrange("p (c i) t -> p c t i", i=4)
+            src = f_raw[:, kh, g, :, 256 * q : 256 * (q + 1)].rearrange("p t (c i) -> p c t i", i=4)
+            if piece in F_ON_V:
                 nc.vector.tensor_copy(out=dst, in_=src)
             else:
                 nc.scalar.copy(out=dst, in_=src)
@@ -271,25 +252,13 @@ def tile_ftn_residual_turn_s9_kernel(tc, lam, amp, h_words, h_scales, y, v, f, o
             nc.vector.tensor_add(out=o[:], in0=d_t[i, kh][:], in1=lam_sb[:, i, cols])
             nc.sync.dma_start(out=out[P * i : P * (i + 1), cols], in_=o[:])
 
-        f_done = [0, 0]
-
-        def f_step(copies, quants):
-            for n in range(copies):
-                if f_done[0] < 16:
-                    f_copy(f_done[0])
-                    f_done[0] += 1
-            for n in range(quants):
-                if 2 * f_done[1] + FQ_LAG < f_done[0] or (f_done[0] == 16 and f_done[1] < 8):
-                    f_quant(f_done[1])
-                    f_done[1] += 1
-
         pending = []
-
         todo = [(i, kh) for i in range(TILES) for kh in range(2)]
+        f_ready = [0]
 
         def second():
             for x in todo:
-                if x[0] in rc_t and f_done[1] >= NG * (x[1] + 1):
+                if x[0] in rc_t and f_ready[0] >= NG * (x[1] + 1):
                     if len(pending) == 2:
                         add(*pending.pop(0))
                     stage2(*x)
@@ -297,74 +266,47 @@ def tile_ftn_residual_turn_s9_kernel(tc, lam, amp, h_words, h_scales, y, v, f, o
                     todo.remove(x)
                     break
 
-        def flush(keep_last=0):
-            while len(pending) > keep_last:
-                add(*pending.pop(0))
-
-        lam_turn(0)
-        lam_turn(1)
-        lam_tanh(0)
-        lam_tanh(1)
+        S = NG * TILES
+        for j in range(2):
+            lam_turn(j)
+            lam_tanh(j)
         x_mul(0)
         x_quant(0)
-        x_mul(1)
-        for s in range(NG):
-            stage1(s)
-        lam_turn(2)
-        lam_tanh(2)
-        for i in range(TILES + 2):
-            if 1 <= i < TILES - 1:
-                x_quant(i + 1)
-            if 1 <= i < TILES - 2:
-                x_mul(i + 2)
-            for b in range(NG):
-                if i < TILES:
-                    sub(NG * i + b)
-                if 1 <= i < TILES - 1:
-                    stage1(NG * (i + 1) + b)
-                if b == 1 and 1 <= i <= TILES:
-                    r_quant(i - 1)
-            if i == 0:
-                x_quant(1)
-                x_mul(2)
-                for b in range(NG):
-                    stage1(NG + b)
-            flush()
-            second()
-            f_step(F_STEPS[0], 1)
-            if i < C_TILES:
-                t_turn(i, 0)
-                t_turn(i, 1)
-                t_mul(i, 0)
-                t_turn(i, 2)
-                f_step(F_STEPS[1], 0)
-                t_mul(i, 1)
-                t_turn(i, 3)
-                t_mul(i, 2)
-                if i + 3 < TILES:
-                    lam_turn(i + 3)
-                    lam_tanh(i + 3)
+        for s in range(-Z, S + 9):
+            if 0 <= s < S:
+                sub(s)
+            if 0 <= s + Z < S:
+                stage1(s + Z)
+            for j in range(1, TILES):
+                if s == NG * j + -10 or (s == -Z and j > 1 and NG * j + -10 < -Z):
+                    if j > 1:
+                        lam_turn(j)
+                        lam_tanh(j)
+                if s == max(NG * j + -8, -Z):
+                    x_mul(j)
+                if s == max(NG * j + -6, -Z + 1):
+                    x_quant(j)
+            if 0 <= s - 2 < S:
+                t_mul(s - 2)
+            if s % 2 == 1 and 0 < s < S:
+                t_turn(s - 1)
+                t_turn(s)
+                t_scale(s - 1)
+                t_scale(s)
+            for j in range(TILES):
+                if s == NG * j + 6:
+                    r_quant(j)
+            if s >= 0:
+                for kg in range(8):
+                    if s == 2 * kg + 3:
+                        f_quant(kg)
+                        f_ready[0] += 1
+                if pending:
+                    add(*pending.pop(0))
                 second()
-                t_mul(i, 3)
-                f_step(F_STEPS[2], 1)
-            elif i < TILES:
-                mul(NG * i)
-                mul(NG * i + 1)
-                r_turn(i, 0)
-                r_copy(i, 0)
-                f_step(F_STEPS[1], 0)
-                if i + 3 < TILES:
-                    lam_turn(i + 3)
-                    lam_tanh(i + 3)
-                mul(NG * i + 2)
-                flush(1)
-                second()
-                mul(NG * i + 3)
-                r_turn(i, 1)
-                r_copy(i, 1)
-                f_step(F_STEPS[2], 1)
-            else:
-                second()
-            second()
-            f_step(F_STEPS[3], 0)
-        flush()
+                if s >= S + 2:
+                    second()
+            if 0 <= s - 0 < 16:
+                f_copy(s - 0)
+        while pending:
+            add(*pending.pop(0))

from contextlib import ExitStack

import concourse.mybir as mybir
from concourse.masks import make_identity

F32 = mybir.dt.float32
BF16 = mybir.dt.bfloat16
I32 = mybir.dt.int32
U32 = mybir.dt.uint32
U8 = mybir.dt.uint8
E4M3X4 = mybir.dt.float8_e4m3fn_x4
E5M2X4 = mybir.dt.float8_e5m2_x4
E2M1X4 = mybir.dt.float4_e2m1fn_x4
ALU = mybir.AluOpType
COPY = mybir.ActivationFunctionType.Copy
TANH = mybir.ActivationFunctionType.Tanh

M, K, N = 1024, 1024, 2048
P = 128
FLOPS = 2 * M * K * N * 2
TILES = M // P
KG = K // 512
NG = N // 512
X_ON_V = 8
F_ON_V = ()
TURN, Z = 3, 3
S_BLOCKS = {3: (1, 3), 4: (0, 1, 2, 3), 5: (0, 1, 2, 3), 6: (0, 1, 2, 3), 7: (0, 1, 2, 3)}
F_STEPS = (1, 1, 1, 1)


def tile_ftn_residual_turn_s9_kernel(tc, lam, amp, h_words, h_scales, y, v, f, out):
    nc = tc.nc
    with ExitStack() as ctx:
        keep = ctx.enter_context(tc.tile_pool(name="keep", bufs=1))
        work = ctx.enter_context(tc.tile_pool(name="work", bufs=2))
        psum = ctx.enter_context(tc.psum_pool(name="psum", bufs=2))

        warm = keep.tile([P, 1], F32)
        nc.vector.memset(warm[:], 0.0)
        warm_out = keep.tile([P, 1], F32)
        nc.scalar.activation(out=warm_out[:], in_=warm[:], func=TANH)
        hs = keep.tile([P, KG, N], U8, align_bytes=64)
        nc.vector.memset(hs[:].rearrange("p g n -> p (g n)").bitcast(I32), 0)
        ident = keep.tile([P, P], F32, align_bytes=64)
        make_identity(nc, ident[:])

        v_turned = keep.tile([P, NG, 4], BF16, align_bytes=64)
        amp_sb = keep.tile([P, KG, 4], BF16, align_bytes=64)
        hw = keep.tile([P, KG, 2 * N], U8, align_bytes=64)
        lam_sb = keep.tile([P, TILES, K], BF16, align_bytes=64)
        f_raw = keep.tile([P, 2, NG, 4, 512], BF16, align_bytes=64)

        y_t = {}

        def load_lam(i):
            nc.sync.dma_start(out=lam_sb[:, i, :], in_=lam[P * i : P * (i + 1), :])

        def load_y(i):
            y_t[i] = work.tile([P, N], BF16, name="y_in", bufs=8, align_bytes=64)
            nc.sync.dma_start(out=y_t[i][:], in_=y[P * i : P * (i + 1), :])

        def load_f(kh, g):
            cols = slice(512 * kh, 512 * (kh + 1))
            nc.sync.dma_start(
                out=f_raw[:, kh, g], in_=f[512 * g : 512 * (g + 1), cols].rearrange("(p j) k -> p j k", j=4)
            )

        def load_h(half):
            cols = slice(N * half, N * (half + 1))
            nc.sync.dma_start(
                out=hw[:, :, cols].bitcast(I32), in_=h_words[:, :, cols].rearrange("g p c -> p g c").bitcast(I32)
            )

        nc.scalar.dma_start(out=amp_sb[:], in_=amp.rearrange("(g p t) -> p g t", g=KG, t=4))
        load_lam(0)
        load_lam(1)
        for q in range(4):
            nc.sync.dma_start(
                out=hs[32 * q : 32 * q + 4].bitcast(I32),
                in_=h_scales[:, 4 * q : 4 * q + 4, :].rearrange("g r n -> r g n").bitcast(I32),
            )
        load_h(0)
        load_y(0)
        load_h(1)
        nc.sync.dma_start(out=v_turned[:], in_=v.rearrange("(g p t) -> p g t", g=NG, t=4))
        load_lam(2)
        load_y(1)
        load_f(0, 0)
        load_f(0, 1)
        load_lam(3)
        load_f(0, 2)
        load_f(0, 3)
        load_y(2)
        load_lam(4)
        for g in range(NG):
            load_f(1, g)
        load_y(3)
        for i in range(5, TILES):
            load_lam(i)
            load_y(i - 1)
        load_y(TILES - 1)

        v_col = keep.tile([P, NG, 4], F32)
        nc.vector.tensor_copy(out=v_col[:], in_=v_turned[:])
        f_codes = keep.tile([P, 2, NG, 512], U32, align_bytes=64)
        f_scales = keep.tile([P, 2, NG, 512], U8, align_bytes=64)

        xt, xf_t, xb_t, xc_t, xs_t = {}, {}, {}, {}, {}
        z_t, t_t, rn_t, rg_t, rc_t, rs_t, d_t, tr_t, fg_t = {}, {}, {}, {}, {}, {}, {}, {}, {}

        def lam_turn(i):
            bank = psum.tile([P, 4, P], F32, name="bank", tag="turn", bufs=TURN)
            words = lam_sb[:, i, :].bitcast(F32)
            for g in range(KG):
                for u in range(2):
                    nc.tensor.transpose(bank[:, 2 * g + u, :], words[:, 256 * g + u : 256 * (g + 1) : 2], ident[:])
            xt[i] = bank

        def lam_tanh(i):
            xf = work.tile([P, KG, P, 4], F32, name="xf", bufs=2, align_bytes=64)
            for g in range(KG):
                nc.scalar.activation(
                    out=xf[:, g].rearrange("p m (u e) -> p m u e", u=2),
                    in_=xt[i][:, 2 * g : 2 * g + 2, :].bitcast(BF16).rearrange("p u (m e) -> p m u e", e=2),
                    func=TANH,
                )
            xf_t[i] = xf

        def x_mul(i):
            engine = nc.vector if i < X_ON_V else nc.gpsimd
            xb = work.tile([P, KG, P, 4], BF16, name="xb", bufs=1, align_bytes=64)
            for g in range(KG):
                engine.tensor_tensor(
                    out=xb[:, g],
                    in0=xf_t[i][:, g],
                    in1=amp_sb[:, g, :].unsqueeze(1).to_broadcast([P, P, 4]),
                    op=ALU.mult,
                )
            xb_t[i] = xb

        def x_quant(i):
            xc = work.tile([P, KG * P], U32, name="xc", bufs=3, align_bytes=64)
            xs = work.tile([P, KG * P], U8, name="xs", bufs=3, align_bytes=64)
            nc.vector.quantize_mx(
                out=xc[:].bitcast(E4M3X4), scales=xs[:], in_=xb_t[i][:].rearrange("p g m t -> p (g m t)")
            )
            xc_t[i], xs_t[i] = xc, xs

        def stage1(s):
            i, b = divmod(s, NG)
            z = psum.tile([P, 512], F32, name="z", tag="z", bufs=Z)
            for g in range(KG):
                nc.tensor.matmul_mx(
                    out=z[:],
                    lhsT=xc_t[i][:, P * g : P * (g + 1)].bitcast(E4M3X4),
                    lhsT_scale=xs_t[i][:, P * g : P * (g + 1)],
                    rhs=hw[:, g, 1024 * b : 1024 * (b + 1)].bitcast(E2M1X4),
                    rhs_scale=hs[:, g, 512 * b : 512 * (b + 1)],
                    start=(g == 0),
                    stop=(g == KG - 1),
                )
            z_t[s] = z

        def sub(s):
            i, b = divmod(s, NG)
            if b == 0:
                t_t[i] = work.tile([P, N], F32, name="t", bufs=5, align_bytes=64)
            cols = slice(512 * b, 512 * (b + 1))
            nc.vector.tensor_sub(
                out=t_t[i][:, cols].rearrange("p (t q) -> p t q", t=4),
                in0=y_t[i][:, cols].rearrange("p (q t) -> p t q", t=4),
                in1=z_t[s][:].rearrange("p (q t) -> p t q", t=4),
            )

        def t_turn(s):
            i, b = divmod(s, NG)
            bank = psum.tile([P, 4, P], F32, name="bank", tag="turn", bufs=TURN)
            for t in range(4):
                nc.tensor.transpose(bank[:, t, :], t_t[i][:, 512 * b + P * t : 512 * b + P * (t + 1)], ident[:])
            tr_t[i, b] = bank

        def t_scale(s):
            i, b = divmod(s, NG)
            if b in S_BLOCKS.get(i, ()):
                rn = work.tile([P, 4, P], BF16, name="rn", bufs=3, align_bytes=64)
                for t in range(4):
                    nc.scalar.activation(out=rn[:, t, :], in_=tr_t[i, b][:, t, :], func=COPY, scale=v_col[:, b, t : t + 1])
                rn_t[s] = rn

        def t_mul(s):
            i, b = divmod(s, NG)
            if b == 0:
                rg_t[i] = work.tile([P, NG, P, 4], BF16, name="rg", bufs=2, align_bytes=64)
            if s in rn_t:
                nc.vector.tensor_copy(
                    out=rg_t[i][:, b].rearrange("p (c i) t -> p c t i", i=4),
                    in_=rn_t[s][:].rearrange("p t (c i) -> p c t i", i=4),
                )
            else:
                nc.vector.tensor_tensor(
                    out=rg_t[i][:, b],
                    in0=tr_t[i, b][:].rearrange("p t m -> p m t"),
                    in1=v_turned[:, b, :].unsqueeze(1).to_broadcast([P, P, 4]),
                    op=ALU.mult,
                )

        def r_quant(i):
            rc = work.tile([P, NG * P], U32, name="rc", bufs=6, align_bytes=64)
            rs = work.tile([P, NG * P], U8, name="rs", bufs=6, align_bytes=64)
            nc.vector.quantize_mx(
                out=rc[:].bitcast(E5M2X4), scales=rs[:], in_=rg_t[i][:].rearrange("p g m t -> p (g m t)")
            )
            rc_t[i], rs_t[i] = rc, rs

        def f_copy(piece):
            kg, q = divmod(piece, 2)
            kh, g = divmod(kg, NG)
            if q == 0:
                fg_t[kg] = work.tile([P, 512, 4], BF16, name="fg", bufs=5, align_bytes=64)
            dst = fg_t[kg][:, 256 * q : 256 * (q + 1), :].rearrange("p (c i) t -> p c t i", i=4)
            src = f_raw[:, kh, g, :, 256 * q : 256 * (q + 1)].rearrange("p t (c i) -> p c t i", i=4)
            if piece in F_ON_V:
                nc.vector.tensor_copy(out=dst, in_=src)
            else:
                nc.scalar.copy(out=dst, in_=src)

        def f_quant(kg):
            kh, g = divmod(kg, NG)
            nc.vector.quantize_mx(
                out=f_codes[:, kh, g, :].bitcast(E4M3X4),
                scales=f_scales[:, kh, g, :],
                in_=fg_t[kg][:].rearrange("p c j -> p (c j)"),
            )

        def stage2(i, kh):
            d = psum.tile([P, 512], F32, name="d", tag="d", bufs=2)
            for g in range(NG):
                nc.tensor.matmul_mx(
                    out=d[:],
                    lhsT=rc_t[i][:, P * g : P * (g + 1)].bitcast(E5M2X4),
                    lhsT_scale=rs_t[i][:, P * g : P * (g + 1)],
                    rhs=f_codes[:, kh, g, :].bitcast(E4M3X4),
                    rhs_scale=f_scales[:, kh, g, :],
                    start=(g == 0),
                    stop=(g == NG - 1),
                )
            d_t[i, kh] = d

        def add(i, kh):
            o = work.tile([P, 512], F32, name="o", bufs=4, align_bytes=64)
            cols = slice(512 * kh, 512 * (kh + 1))
            nc.vector.tensor_add(out=o[:], in0=d_t[i, kh][:], in1=lam_sb[:, i, cols])
            nc.sync.dma_start(out=out[P * i : P * (i + 1), cols], in_=o[:])

        pending = []
        todo = [(i, kh) for i in range(TILES) for kh in range(2)]
        f_ready = [0]

        def second():
            for x in todo:
                if x[0] in rc_t and f_ready[0] >= NG * (x[1] + 1):
                    if len(pending) == 2:
                        add(*pending.pop(0))
                    stage2(*x)
                    pending.append(x)
                    todo.remove(x)
                    break

        S = NG * TILES
        for j in range(2):
            lam_turn(j)
            lam_tanh(j)
        x_mul(0)
        x_quant(0)
        for s in range(-Z, S + 9):
            if 0 <= s < S:
                sub(s)
            if 0 <= s + Z < S:
                stage1(s + Z)
            for j in range(1, TILES):
                if s == NG * j + -10 or (s == -Z and j > 1 and NG * j + -10 < -Z):
                    if j > 1:
                        lam_turn(j)
                        lam_tanh(j)
                if s == max(NG * j + -8, -Z):
                    x_mul(j)
                if s == max(NG * j + -6, -Z + 1):
                    x_quant(j)
            if 0 <= s - 2 < S:
                t_mul(s - 2)
            if s % 2 == 1 and 0 < s < S:
                t_turn(s - 1)
                t_turn(s)
                t_scale(s - 1)
                t_scale(s)
            for j in range(TILES):
                if s == NG * j + 6:
                    r_quant(j)
            if s >= 0:
                for kg in range(8):
                    if s == 2 * kg + 3:
                        f_quant(kg)
                        f_ready[0] += 1
                if pending:
                    add(*pending.pop(0))
                second()
                if s >= S + 2:
                    second()
            if 0 <= s - 0 < 16:
                f_copy(s - 0)
        while pending:
            add(*pending.pop(0))
